import numpy as np
import ml_dtypes


def mxq(x, axis, fmt="e4m3"):
    dtype, down = {"e4m3": (ml_dtypes.float8_e4m3fn, 7), "e5m2": (ml_dtypes.float8_e5m2, 14)}[fmt]
    v = np.moveaxis(np.asarray(x, np.float32).astype(ml_dtypes.bfloat16).astype(np.float64), axis, -1)
    blocks = v.reshape(v.shape[:-1] + (-1, 32))
    amax = np.abs(blocks).max(-1, keepdims=True)
    byte = np.maximum(np.where(amax > 0, np.frexp(amax)[1] - 1 + 127, 0) - down, 1)
    scale = np.exp2(byte - 127.0)
    codes = (blocks / scale).astype(np.float32).astype(dtype).astype(np.float64)
    return np.moveaxis((codes * scale).reshape(v.shape), -1, axis)


WIDE = False


def mx_kscale(k):
    if not WIDE:
        return np.ones(k)
    levels = np.array([10, -10, 5, -5, 0])
    if k % 512:
        return np.exp2(np.random.permutation(np.resize(levels, k // 32))).repeat(32)
    a = np.empty((k // 512, 16))
    for p in range(k // 512):
        a[p, :8] = np.random.permutation(np.resize(levels, 8))
        for g in range(8):
            far = levels[np.abs(levels - a[p, g]) >= 10]
            a[p, g + 8] = far[np.random.randint(len(far))]
    return np.exp2(a.ravel()).repeat(32)


def f64(x):
    return np.asarray(x).astype(np.float64)


def striped(idx):
    return np.tile(idx.reshape(-1, 16).T, (8, 1)).astype(np.uint16)


def unstriped(offs):
    return offs[:16].T.reshape(-1).astype(np.int64)


E2M1 = np.array([0.0, 0.5, 1.0, 1.5, 2.0, 3.0, 4.0, 6.0, -0.0, -0.5, -1.0, -1.5, -2.0, -3.0, -4.0, -6.0])


def pack_weight(w, fmt):
    k, n = w.shape
    w = f64(np.asarray(w, np.float32).astype(ml_dtypes.bfloat16)).reshape(k // 32, 32, n)
    amax = np.abs(w).max(1)
    if fmt == "e4m3":
        byte = np.frexp(amax)[1] - 1 + 127 - 7
    else:
        mant, ex = np.frexp(amax / 6.0)
        byte = np.where(mant > 0.5, ex, ex - 1) + 127
    byte = np.clip(np.where(amax > 0, byte, 1), 1, 254)
    scaled = (w * np.exp2(127.0 - byte)[:, None, :]).reshape(k, n).astype(np.float32)
    by_word = np.ascontiguousarray(scaled.reshape(k // 512, 128, 4, n).transpose(0, 1, 3, 2))
    if fmt == "e4m3":
        words = by_word.astype(ml_dtypes.float8_e4m3fn).view(np.uint8)
    else:
        c = by_word.astype(ml_dtypes.float4_e2m1fn).view(np.uint8) & 0xF
        words = (c[..., 0::2] | (c[..., 1::2] << 4)).reshape(k // 512, 128, 2 * n)
    return np.ascontiguousarray(words), np.ascontiguousarray(byte.astype(np.uint8).reshape(k // 512, 16, n))


def unpack_weight(words, scales, fmt):
    g, _, n = scales.shape
    words = np.ascontiguousarray(words).reshape(g, 128, n, -1)
    if fmt == "e4m3":
        vals = words.view(ml_dtypes.float8_e4m3fn).astype(np.float64)
    else:
        nib = np.empty((g, 128, n, 4), np.uint8)
        nib[..., 0::2] = words & 0xF
        nib[..., 1::2] = words >> 4
        vals = E2M1[nib]
    vals = vals * np.repeat(np.exp2(scales.astype(np.float64) - 127.0), 8, axis=1)[..., None]
    return vals.transpose(0, 1, 3, 2).reshape(g * 512, n)


def gelu(v):
    return 0.5 * v * (1.0 + np.tanh(np.sqrt(2.0 / np.pi) * (v + 0.044715 * v**3)))


K, K2, H, N, T, T3, S, T2, P = 1024, 512, 1024, 512, 2048, 1024, 512, 2048, 1024

def setup_inputs():
    n = np.random.standard_normal
    s, s2, u = mx_kscale(K)[:, None], mx_kscale(K2)[:, None], mx_kscale(H)[:, None]
    d = {}
    d["tab_words"], d["tab_scales"] = pack_weight(n((K, T)) * s, "e4m3")
    d["offs"] = striped(np.random.permutation(T)[:S])
    d["tab2_words"], d["tab2_scales"] = pack_weight(n((K2, T3)) * s2, "e4m3")
    d["offs2"] = striped(np.random.permutation(T3)[:S])
    d["w1_words"], d["w1_scales"] = pack_weight(n((K, H)) / K ** 0.5 / s, "e2m1")
    d["g1"] = (1.4 * np.exp(0.4 * n(H)) * u[:, 0]).astype(np.float32)
    d["w2"] = (1.6 * n((K2, H)) / K2 ** 0.5 / s2).astype(np.float32)
    d["rest"] = (0.8 * n(H)).astype(np.float32)
    d["g2"] = (1.6 * np.exp(0.3 * n(H)) * u[:, 0]).astype(np.float32)
    d["page0"] = (n((H, T2)) * u).astype(np.float32)
    perm = np.random.permutation(T2)
    d["offs3"] = striped(perm[:S])
    d["offs4"] = striped(perm[S:2 * S])
    d["wg1"] = np.exp(0.3 * n((128, S))).astype(np.float32)
    d["wg2"] = np.exp(0.3 * n((128, S))).astype(np.float32)
    d["offs5"] = striped(np.random.permutation(T2)[:P])
    d["bv"] = ((0.4 * n(H) - 0.8) * u[:, 0]).astype(np.float32)
    d["gi"] = (1.6 * np.exp(0.3 * n(H)) / u[:, 0]).astype(np.float32)
    d["go"] = (np.exp(0.3 * n(H)) * u[:, 0]).astype(np.float32)
    d["wa"] = (n((H, N)) / H ** 0.5 / u).astype(np.float32)
    d["wb_words"], d["wb_scales"] = pack_weight(1.2 * n((H, N)) / H ** 0.5 / u, "e4m3")
    return d

def reference(tab_words, tab_scales, offs, tab2_words, tab2_scales, offs2, w1_words, w1_scales, g1, w2, rest, g2, page0, offs3, offs4, wg1, wg2, offs5, bv, gi, go, wa, wb_words, wb_scales):
    v = unpack_weight(tab_words, tab_scales, "e4m3")[:, unstriped(offs)]
    v2 = unpack_weight(tab2_words, tab2_scales, "e4m3")[:, unstriped(offs2)]
    h1 = f64(g1)[:, None] * (unpack_weight(w1_words, w1_scales, "e2m1").T @ v)
    h2 = f64(g2)[:, None] * np.tanh((mxq(f64(w2), 0, "e4m3").T @ v2) - f64(rest)[:, None])
    page = f64(page0).copy()
    page[:, unstriped(offs3)] = np.tile(f64(wg1), (H // 128, 1)) * h1
    page[:, unstriped(offs4)] = np.tile(f64(wg2), (H // 128, 1)) * h2
    x = np.abs(page[:, unstriped(offs5)]) + f64(bv)[:, None]
    bent = f64(go)[:, None] * np.tanh(f64(gi)[:, None] * x)
    ya = mxq(f64(wa), 0, "e4m3").T @ mxq(x, 0, "e4m3")
    yb = unpack_weight(wb_words, wb_scales, "e4m3").T @ mxq(bent, 0, "e4m3")
    return np.maximum(ya, yb)

@@ -1,0 +1,325 @@
+from contextlib import ExitStack
+
+import concourse.mybir as mybir
+
+K, K2, H, N, T, T3, S, T2, R = 1024, 512, 1024, 512, 2048, 1024, 512, 2048, 1024
+FLOPS = 2 * S * H * (K + K2) + 2 * 2 * H * N * R
+
+F32 = mybir.dt.float32
+BF16 = mybir.dt.bfloat16
+I32 = mybir.dt.int32
+U32 = mybir.dt.uint32
+U16 = mybir.dt.uint16
+U8 = mybir.dt.uint8
+FP8X4 = mybir.dt.float8_e4m3fn_x4
+FP4X4 = mybir.dt.float4_e2m1fn_x4
+ACT = mybir.ActivationFunctionType
+ALU = mybir.AluOpType
+
+P = 128
+PACK = 4
+KP = P * PACK
+SLABS = H // P
+QW = 256
+QUARTERS = R // QW
+RUN = 4
+HALF = KP // 2
+
+
+def tile_list_capsule_segment_reading_kernel(
+    tc, tab_words, tab_scales, offs, tab2_words, tab2_scales, offs2, w1_words, w1_scales, g1, w2, rest, g2,
+    page0, offs3, offs4, wg1, wg2, offs5, bv, gi, go, wa, wb_words, wb_scales, out,
+):
+    nc = tc.nc
+    with ExitStack() as ctx:
+        keep = ctx.enter_context(tc.tile_pool(name="keep", bufs=1))
+        ring = ctx.enter_context(tc.tile_pool(name="ring", bufs=2))
+        pages = ctx.enter_context(tc.tile_pool(name="pages", bufs=4))
+        psum = ctx.enter_context(tc.psum_pool(name="psum", bufs=1))
+
+        def held(name, shape, dtype):
+            return keep.tile(shape, dtype, name=name, align_bytes=64)
+
+        def bank(i):
+            return psum.tile([P, 512], F32, name="bank%d" % i)
+
+        def load_list(name, src):
+            t = keep.tile(list(src.shape), U16, name=name)
+            nc.sync.dma_start(t[:], src)
+            return t
+
+        def scale_tile(name, src, engine):
+            t = held(name, [P, src.shape[0], src.shape[2]], U8)
+            engine.memset(t[:].bitcast(I32), 0)
+            return t
+
+        def load_scales(t, src, queue):
+            rows = src.bitcast(I32).rearrange("a (q r) c -> r q a c", r=4)
+            for r in range(4):
+                queue.dma_start(t[r:P:32, :, :].bitcast(I32), rows[r])
+
+        def load_words(name, src):
+            t = held(name, [P, src.shape[1]], U32)
+            nc.sync.dma_start(t[:].bitcast(I32), src.rearrange("p n i -> p (n i)").bitcast(I32))
+            return t
+
+        def load_rows(name, src):
+            t = held(name, [P, 2, PACK], F32)
+            nc.sync.dma_start(t[:], src.rearrange("(b p t) -> p b t", b=2, t=PACK))
+            return t
+
+        def load_wg(name, src, half):
+            t = held(name, [P, 2, S], F32)
+            rows = src.rearrange("(q t) j -> q t j", t=PACK)[:, 2 * half : 2 * half + 2, :]
+            for quad in range(4):
+                nc.sync.dma_start(t[32 * quad : 32 * quad + 32, :, :], rows)
+            return t
+
+        def load_page(s):
+            t = pages.tile([P, T2], F32, name="page")
+            nc.sync.dma_start(t[:], page0.rearrange("(b p t) c -> b t p c", b=2, t=PACK)[s // PACK, s % PACK])
+            return t
+
+        def load_raw(name, src):
+            t = held(name, [P, PACK, src.shape[1]], F32)
+            nc.sync.dma_start(t[:], src.rearrange("(p j) c -> p j c", j=PACK))
+            return t
+
+        w1_sc_raw = scale_tile("w1_sc_raw", w1_scales, nc.vector)
+        tab_sc = scale_tile("tab_sc", tab_scales, nc.vector)
+        tab2_sc = scale_tile("tab2_sc", tab2_scales, nc.gpsimd)
+        wb_sc = scale_tile("wb_sc", wb_scales, nc.gpsimd)
+
+        idx = load_list("idx", offs)
+        load_scales(w1_sc_raw, w1_scales, nc.scalar)
+        w1_raw = held("w1_raw", [P, 2, H], U16)
+        nc.sync.dma_start(w1_raw[:].bitcast(I32), w1_words.rearrange("a p c -> p a c").bitcast(I32))
+        tab_w = [load_words("tab_w0", tab_words[0])]
+        load_scales(tab_sc, tab_scales, nc.scalar)
+        tab_w.append(load_words("tab_w1", tab_words[1]))
+        idx2 = load_list("idx2", offs2)
+        load_scales(tab2_sc, tab2_scales, nc.scalar)
+        tab2_w = load_words("tab2_w", tab2_words[0])
+        g1_t = load_rows("g1_t", g1)
+        idx3 = load_list("idx3", offs3)
+        wg1_t = [load_wg("wg1_lo", wg1, 0)]
+        page = [load_page(0)]
+        rest_t = load_rows("rest_t", rest)
+        g2_t = load_rows("g2_t", g2)
+        w2_raw = [load_raw("w2_raw%d" % i, w2[:, HALF * i : HALF * (i + 1)]) for i in range(2)]
+        idx4 = load_list("idx4", offs4)
+        wg2_t = [load_wg("wg2_lo", wg2, 0)]
+        page.append(load_page(1))
+        idx5 = load_list("idx5", offs5)
+        bv_t = load_rows("bv_t", bv)
+        gi_t = load_rows("gi_t", gi)
+        go_t = load_rows("go_t", go)
+        w2_raw.extend([load_raw("w2_raw%d" % i, w2[:, HALF * i : HALF * (i + 1)]) for i in range(2, 4)])
+        page.append(load_page(2))
+        wg1_t.append(load_wg("wg1_hi", wg1, 1))
+        wg2_t.append(load_wg("wg2_hi", wg2, 1))
+        page.append(load_page(3))
+        wa_raw = [load_raw("x_planes1", wa[0:KP, :]), load_raw("bent_planes1", wa[KP : 2 * KP, :])]
+        load_scales(wb_sc, wb_scales, nc.sync)
+        wb_w = [load_words("wb_w%d" % a, wb_words[a]) for a in range(2)]
+
+        w1_w = held("w1_w", [P, 2, H], U16)
+        w1_sc = held("w1_sc", [P, 2, H], U8)
+        for dst, src in ((w1_w, w1_raw), (w1_sc, w1_sc_raw)):
+            nc.vector.tensor_copy(
+                dst[:].rearrange("p a (b t q) -> p (a b) t q", b=2, t=PACK),
+                src[:].rearrange("p a (b q t) -> p (a b) t q", b=2, t=PACK),
+            )
+        v_w, v_sc = [], []
+        for a in range(2):
+            v_sc.append(held("v_sc%d" % a, [P, S], U8))
+            nc.vector.tensor_copy(v_sc[a][:], tab_sc[:, a, :].indirect(idx[:]))
+            v_w.append(held("v_w%d" % a, [P, S], U32))
+            nc.vector.tensor_copy(v_w[a][:], tab_w[a][:].indirect(idx[:]))
+        v2_sc = held("v2_sc", [P, S], U8)
+        v2_w = held("v2_w", [P, S], U32)
+        nc.vector.tensor_copy(v2_sc[:], tab2_sc[:, 0, :].indirect(idx2[:]))
+        nc.vector.tensor_copy(v2_w[:], tab2_w[:].indirect(idx2[:]))
+        neg_rest = held("neg_rest", [P, 2, PACK], F32)
+        nc.vector.tensor_scalar(neg_rest[:], rest_t[:], -1.0, None, ALU.mult)
+        gi_bv = held("gi_bv", [P, 2, PACK], F32)
+        nc.vector.tensor_tensor(gi_bv[:], gi_t[:], bv_t[:], ALU.mult)
+
+        def col(t, s):
+            return t[:, s // PACK, s % PACK : s % PACK + 1]
+
+        def quantize(name, grouped, width):
+            codes = held(name + "_w", [P, width], U32)
+            scales = held(name + "_sc", [P, width], U8)
+            nc.vector.quantize_mx(out=codes[:].bitcast(FP8X4), scales=scales[:], in_=grouped[:])
+            return codes, scales
+
+        def quantize_w2(b):
+            grouped = ring.tile([P, PACK * KP], BF16, name="grouped_w", align_bytes=64)
+            for i in range(2):
+                nc.scalar.copy(
+                    grouped[:].rearrange("p (t i m j) -> p i m j t", t=PACK, i=2, j=PACK)[:, i],
+                    w2_raw[2 * b + i][:].rearrange("p j (m t) -> p m j t", t=PACK),
+                )
+            return quantize("w2_%d" % b, grouped, KP)
+
+        def quantize_wa(a):
+            grouped = ring.tile([P, PACK * KP], BF16, name="grouped_w", align_bytes=64)
+            nc.scalar.copy(
+                grouped[:].rearrange("p (c i j) -> p c j i", i=RUN, j=PACK),
+                wa_raw[a][:].rearrange("p j (c i) -> p c j i", i=RUN),
+            )
+            return quantize("wa_%d" % a, grouped, KP)
+
+        turn = [0]
+
+        def next_bank():
+            turn.append(turn[-1] + 1)
+            return bank(turn[-1] % 4)
+
+        def put_h1(s, h1):
+            acc = next_bank()
+            cols = slice(P * s, P * s + P)
+            for a in range(2):
+                nc.tensor.matmul_mx(
+                    out=acc[:], lhsT=w1_w[:, a, cols].bitcast(FP4X4), lhsT_scale=w1_sc[:, a, cols],
+                    rhs=v_w[a][:].bitcast(FP8X4), rhs_scale=v_sc[a][:], start=(a == 0), stop=(a == 1),
+                )
+            nc.scalar.activation(h1, acc[:], ACT.Copy, scale=col(g1_t, s))
+            t = s % PACK
+            nc.vector.tensor_tensor(page[s][:].indirect(idx3[:]), h1, wg1_t[t // 2][:, t % 2, :], ALU.mult)
+
+        def put_h2(s, h2):
+            acc = next_bank()
+            t = s % PACK
+            codes, scales = w2_q[s // PACK]
+            cols = slice(P * t, P * t + P)
+            nc.tensor.matmul_mx(
+                out=acc[:], lhsT=codes[:, cols].bitcast(FP8X4), lhsT_scale=scales[:, cols],
+                rhs=v2_w[:].bitcast(FP8X4), rhs_scale=v2_sc[:], start=True, stop=True,
+            )
+            th = keep.tile([P, S], F32, name="th")
+            nc.scalar.activation(th[:], acc[:], ACT.Tanh, bias=col(neg_rest, s))
+            nc.scalar.activation(h2, th[:], ACT.Copy, scale=col(g2_t, s))
+            nc.vector.tensor_tensor(page[s][:].indirect(idx4[:]), h2, wg2_t[t // 2][:, t % 2, :], ALU.mult)
+
+        x_planes = [held("x_planes0", [P, QUARTERS, PACK, QW], BF16)]
+        bent_planes = [held("bent_planes0", [P, QUARTERS, PACK, QW], BF16)]
+
+        def fetch(s, picked, q0, q1):
+            nc.vector.tensor_copy(
+                picked[:, QW * q0 : QW * q1], page[s][:].indirect(idx5[:, QW // 16 * q0 : QW // 16 * q1])
+            )
+
+        def magnitude(picked, mag, q0, q1):
+            nc.scalar.activation(mag[:, QW * q0 : QW * q1], picked[:, QW * q0 : QW * q1], ACT.Abs)
+
+        def features(s, mag, bend, q0, q1):
+            b, t = divmod(s, PACK)
+            cols = slice(QW * q0, QW * q1)
+            if s == SLABS - 1:
+                nc.vector.tensor_scalar(x_planes[b][:, q0, t, :], mag[:, cols], col(bv_t, s), None, ALU.add)
+            else:
+                nc.scalar.activation(
+                    x_planes[b][:, q0:q1, t, :], mag[:, cols].rearrange("p (q c) -> p q c", c=QW), ACT.Identity,
+                    bias=col(bv_t, s),
+                )
+            nc.scalar.activation(bend[:, cols], mag[:, cols], ACT.Tanh, bias=col(gi_bv, s), scale=col(gi_t, s))
+            nc.scalar.activation(
+                bent_planes[b][:, q0:q1, t, :], bend[:, cols].rearrange("p (q c) -> p q c", c=QW), ACT.Copy,
+                scale=col(go_t, s),
+            )
+
+        def weave(name, planes, q, copy):
+            grouped = ring.tile([P, PACK * QW], BF16, name="grouped_" + name[0], align_bytes=64, bufs=4)
+            copy(
+                grouped[:].rearrange("p (c i t) -> p c t i", i=RUN, t=PACK),
+                planes[:, q, :, :].rearrange("p t (c i) -> p c t i", i=RUN),
+            )
+            return quantize(name, grouped, QW)
+
+        x_q, bent_q, w2_q, wa_q = {}, {}, {}, {}
+
+        def weave_first_pass(q):
+            x_q[0, q] = weave("x0_%d" % q, x_planes[0], q, nc.scalar.copy)
+            bent_q[0, q] = weave("b0_%d" % q, bent_planes[0], q, nc.scalar.copy)
+
+        def fresh(name):
+            return keep.tile([P, R], F32, name=name)
+
+        def area(s, role):
+            return fresh("area%d" % (2 * (s % 2) + (s // 2 + role) % 2))
+
+        first = keep.tile([P, S], F32, name="first")
+        put_h1(0, first[:])
+        w2_q[0] = quantize_w2(0)
+        picked = {}
+
+        def put(s):
+            h = area(s, 1)
+            if s == SLABS - 1:
+                put_h1(s, h[:, S:])
+            put_h2(s, h[:, :S])
+            if s + 1 < SLABS - 1:
+                put_h1(s + 1, h[:, S:])
+
+        def fetch_slab(s):
+            picked[s] = area(s, 0)
+            for q0, q1 in [(0, QUARTERS)] if s < SLABS - 1 else [(q, q + 1) for q in range(QUARTERS)]:
+                fetch(s, picked[s], q0, q1)
+            if s + 4 < SLABS:
+                page.append(load_page(s + 4))
+
+        for s in range(2):
+            put(s)
+            fetch_slab(s)
+        w2_q[1] = quantize_w2(1)
+        wa_q[0] = quantize_wa(0)
+        wa_q[1] = quantize_wa(1)
+        x_planes.append(held("x_planes1", [P, QUARTERS, PACK, QW], BF16))
+        bent_planes.append(held("bent_planes1", [P, QUARTERS, PACK, QW], BF16))
+        for s in range(SLABS - 1):
+            mag, bend = area(s, 1), fresh("bend")
+            magnitude(picked[s], mag, 0, QUARTERS)
+            if s + 2 < SLABS:
+                put(s + 2)
+            features(s, mag, bend, 0, QUARTERS)
+            if s + 2 < SLABS:
+                fetch_slab(s + 2)
+            for q in {3: [0, 1], 4: [2], 5: [3]}.get(s, []):
+                weave_first_pass(q)
+
+        out_v = out.rearrange("(n p) j -> p n j", p=P)
+        last = SLABS - 1
+        mag, bend = area(last, 1), fresh("bend")
+
+        def passes(acc, w_codes, w_scales, moving, pair, b):
+            for i in range(2):
+                cols = slice(P * (2 * pair + i), P * (2 * pair + i + 1))
+                nc.tensor.matmul_mx(
+                    out=acc[:, QW * i : QW * (i + 1)], lhsT=w_codes[:, cols].bitcast(FP8X4), lhsT_scale=w_scales[:, cols],
+                    rhs=moving[0][:].bitcast(FP8X4), rhs_scale=moving[1][:],
+                    start=(b == 0 and i == 0), stop=(b == 1 and i == 1),
+                )
+
+        for q in range(QUARTERS):
+            ya = [bank(4 * (q % 2) + pair) for pair in range(2)]
+            yb = [bank(4 * (q % 2) + 2 + pair) for pair in range(2)]
+            for pair in range(2):
+                passes(ya[pair], wa_q[0][0], wa_q[0][1], x_q[0, q], pair, 0)
+                passes(yb[pair], wb_w[0], wb_sc[:, 0, :], bent_q[0, q], pair, 0)
+            magnitude(picked[last], mag, q, q + 1)
+            features(last, mag, bend, q, q + 1)
+            x_q[1, q] = weave("x1_%d" % q, x_planes[1], q, nc.scalar.copy)
+            bent_q[1, q] = weave("b1_%d" % q, bent_planes[1], q, nc.vector.tensor_copy)
+            for pair in range(2):
+                passes(ya[pair], wa_q[1][0], wa_q[1][1], x_q[1, q], pair, 1)
+                passes(yb[pair], wb_w[1], wb_sc[:, 1, :], bent_q[1, q], pair, 1)
+            for pair in range(2):
+                left = ring.tile([P, 2 * QW], F32, name="left")
+                nc.scalar.copy(left[:], ya[pair][:])
+                res = ring.tile([P, 2 * QW], F32, name="res", bufs=3)
+                nc.vector.tensor_tensor(res[:], yb[pair][:], left[:], ALU.max)
+                nc.sync.dma_start(
+                    out_v[:, 2 * pair : 2 * pair + 2, QW * q : QW * (q + 1)], res[:].rearrange("p (n c) -> p n c", n=2)
+                )

@@ -53,10 +53,10 @@ def tile_list_capsule_segment_reading_kernel(
             engine.memset(t[:].bitcast(I32), 0)
             return t
 
-        def load_scales(t, src, queue):
+        def load_scales(t, src):
             rows = src.bitcast(I32).rearrange("a (q r) c -> r q a c", r=4)
             for r in range(4):
-                queue.dma_start(t[r:P:32, :, :].bitcast(I32), rows[r])
+                nc.sync.dma_start(t[r:P:32, :, :].bitcast(I32), rows[r])
 
         def load_words(name, src):
             t = held(name, [P, src.shape[1]], U32)
@@ -85,65 +85,45 @@ def tile_list_capsule_segment_reading_kernel(
             nc.sync.dma_start(t[:], src.rearrange("(p j) c -> p j c", j=PACK))
             return t
 
+        tab2_sc = scale_tile("tab2_sc", tab2_scales, nc.vector)
         w1_sc_raw = scale_tile("w1_sc_raw", w1_scales, nc.vector)
-        tab_sc = scale_tile("tab_sc", tab_scales, nc.vector)
-        tab2_sc = scale_tile("tab2_sc", tab2_scales, nc.gpsimd)
+        tab_sc = scale_tile("tab_sc", tab_scales, nc.gpsimd)
         wb_sc = scale_tile("wb_sc", wb_scales, nc.gpsimd)
 
-        idx = load_list("idx", offs)
-        load_scales(w1_sc_raw, w1_scales, nc.scalar)
+        tab2_w = load_words("tab2_w", tab2_words[0])
+        idx2 = load_list("idx2", offs2)
+        load_scales(tab2_sc, tab2_scales)
+        w2_raw = [load_raw("w2_raw0", w2[:, :HALF])]
         w1_raw = held("w1_raw", [P, 2, H], U16)
         nc.sync.dma_start(w1_raw[:].bitcast(I32), w1_words.rearrange("a p c -> p a c").bitcast(I32))
-        tab_w = [load_words("tab_w0", tab_words[0])]
-        load_scales(tab_sc, tab_scales, nc.scalar)
-        tab_w.append(load_words("tab_w1", tab_words[1]))
-        idx2 = load_list("idx2", offs2)
-        load_scales(tab2_sc, tab2_scales, nc.scalar)
-        tab2_w = load_words("tab2_w", tab2_words[0])
-        g1_t = load_rows("g1_t", g1)
-        idx3 = load_list("idx3", offs3)
-        wg1_t = [load_wg("wg1_lo", wg1, 0)]
+        w2_raw.append(load_raw("w2_raw1", w2[:, HALF : 2 * HALF]))
+        load_scales(w1_sc_raw, w1_scales)
         page = [load_page(0)]
         rest_t = load_rows("rest_t", rest)
         g2_t = load_rows("g2_t", g2)
-        w2_raw = [load_raw("w2_raw%d" % i, w2[:, HALF * i : HALF * (i + 1)]) for i in range(2)]
         idx4 = load_list("idx4", offs4)
         wg2_t = [load_wg("wg2_lo", wg2, 0)]
+        tab_w = [load_words("tab_w0", tab_words[0])]
+        idx = load_list("idx", offs)
+        load_scales(tab_sc, tab_scales)
+        tab_w.append(load_words("tab_w1", tab_words[1]))
+        g1_t = load_rows("g1_t", g1)
         page.append(load_page(1))
+        idx3 = load_list("idx3", offs3)
+        wg1_t = [load_wg("wg1_lo", wg1, 0)]
         idx5 = load_list("idx5", offs5)
+        w2_raw.append(load_raw("w2_raw2", w2[:, 2 * HALF : 3 * HALF]))
+        w2_raw.append(load_raw("area0", w2[:, 3 * HALF :]))
         bv_t = load_rows("bv_t", bv)
         gi_t = load_rows("gi_t", gi)
         go_t = load_rows("go_t", go)
-        w2_raw.extend([load_raw("w2_raw%d" % i, w2[:, HALF * i : HALF * (i + 1)]) for i in range(2, 4)])
         page.append(load_page(2))
-        wg1_t.append(load_wg("wg1_hi", wg1, 1))
         wg2_t.append(load_wg("wg2_hi", wg2, 1))
+        wg1_t.append(load_wg("wg1_hi", wg1, 1))
         page.append(load_page(3))
         wa_raw = [load_raw("x_planes1", wa[0:KP, :]), load_raw("bent_planes1", wa[KP : 2 * KP, :])]
-        load_scales(wb_sc, wb_scales, nc.sync)
+        load_scales(wb_sc, wb_scales)
         wb_w = [load_words("wb_w%d" % a, wb_words[a]) for a in range(2)]
-
-        w1_w = held("w1_w", [P, 2, H], U16)
-        w1_sc = held("w1_sc", [P, 2, H], U8)
-        for dst, src in ((w1_w, w1_raw), (w1_sc, w1_sc_raw)):
-            nc.vector.tensor_copy(
-                dst[:].rearrange("p a (b t q) -> p (a b) t q", b=2, t=PACK),
-                src[:].rearrange("p a (b q t) -> p (a b) t q", b=2, t=PACK),
-            )
-        v_w, v_sc = [], []
-        for a in range(2):
-            v_sc.append(held("v_sc%d" % a, [P, S], U8))
-            nc.vector.tensor_copy(v_sc[a][:], tab_sc[:, a, :].indirect(idx[:]))
-            v_w.append(held("v_w%d" % a, [P, S], U32))
-            nc.vector.tensor_copy(v_w[a][:], tab_w[a][:].indirect(idx[:]))
-        v2_sc = held("v2_sc", [P, S], U8)
-        v2_w = held("v2_w", [P, S], U32)
-        nc.vector.tensor_copy(v2_sc[:], tab2_sc[:, 0, :].indirect(idx2[:]))
-        nc.vector.tensor_copy(v2_w[:], tab2_w[:].indirect(idx2[:]))
-        neg_rest = held("neg_rest", [P, 2, PACK], F32)
-        nc.vector.tensor_scalar(neg_rest[:], rest_t[:], -1.0, None, ALU.mult)
-        gi_bv = held("gi_bv", [P, 2, PACK], F32)
-        nc.vector.tensor_tensor(gi_bv[:], gi_t[:], bv_t[:], ALU.mult)
 
         def col(t, s):
             return t[:, s // PACK, s % PACK : s % PACK + 1]
@@ -151,25 +131,25 @@ def tile_list_capsule_segment_reading_kernel(
         def quantize(name, grouped, width):
             codes = held(name + "_w", [P, width], U32)
             scales = held(name + "_sc", [P, width], U8)
-            nc.vector.quantize_mx(out=codes[:].bitcast(FP8X4), scales=scales[:], in_=grouped[:])
+            nc.vector.quantize_mx(out=codes[:].bitcast(FP8X4), scales=scales[:], in_=grouped)
             return codes, scales
 
         def quantize_w2(b):
-            grouped = ring.tile([P, PACK * KP], BF16, name="grouped_w", align_bytes=64)
+            grouped = held("w2_grouped%d" % b, [P, PACK * KP], BF16)
             for i in range(2):
                 nc.scalar.copy(
                     grouped[:].rearrange("p (t i m j) -> p i m j t", t=PACK, i=2, j=PACK)[:, i],
                     w2_raw[2 * b + i][:].rearrange("p j (m t) -> p m j t", t=PACK),
                 )
-            return quantize("w2_%d" % b, grouped, KP)
+            return quantize("w2_%d" % b, grouped[:], KP)
 
-        def quantize_wa(a):
-            grouped = ring.tile([P, PACK * KP], BF16, name="grouped_w", align_bytes=64)
+        def round_wa(a):
+            grouped = held("wa_grouped%d" % a, [P, PACK * KP], BF16)
             nc.scalar.copy(
                 grouped[:].rearrange("p (c i j) -> p c j i", i=RUN, j=PACK),
                 wa_raw[a][:].rearrange("p j (c i) -> p c j i", i=RUN),
             )
-            return quantize("wa_%d" % a, grouped, KP)
+            return grouped
 
         turn = [0]
 
@@ -217,7 +197,7 @@ def tile_list_capsule_segment_reading_kernel(
         def features(s, mag, bend, q0, q1):
             b, t = divmod(s, PACK)
             cols = slice(QW * q0, QW * q1)
-            if s == SLABS - 1:
+            if s == SLABS - 1 and q0 > 0:
                 nc.vector.tensor_scalar(x_planes[b][:, q0, t, :], mag[:, cols], col(bv_t, s), None, ALU.add)
             else:
                 nc.scalar.activation(
@@ -230,38 +210,63 @@ def tile_list_capsule_segment_reading_kernel(
                 scale=col(go_t, s),
             )
 
-        def weave(name, planes, q, copy):
+        def weave(name, planes, q, copy, c0=0, width=QW):
             grouped = ring.tile([P, PACK * QW], BF16, name="grouped_" + name[0], align_bytes=64, bufs=4)
             copy(
-                grouped[:].rearrange("p (c i t) -> p c t i", i=RUN, t=PACK),
-                planes[:, q, :, :].rearrange("p t (c i) -> p c t i", i=RUN),
+                grouped[:, : PACK * width].rearrange("p (c i t) -> p c t i", i=RUN, t=PACK),
+                planes[:, q, :, c0 : c0 + width].rearrange("p t (c i) -> p c t i", i=RUN),
             )
-            return quantize(name, grouped, QW)
+            return quantize(name, grouped[:, : PACK * width], width)
 
-        x_q, bent_q, w2_q, wa_q = {}, {}, {}, {}
+        x_q, bent_q, w2_q = {}, {}, {}
 
         def weave_first_pass(q):
             x_q[0, q] = weave("x0_%d" % q, x_planes[0], q, nc.scalar.copy)
             bent_q[0, q] = weave("b0_%d" % q, bent_planes[0], q, nc.scalar.copy)
 
         def fresh(name):
-            return keep.tile([P, R], F32, name=name)
+            return held(name, [P, R], F32)
 
         def area(s, role):
             return fresh("area%d" % (2 * (s % 2) + (s // 2 + role) % 2))
 
-        first = keep.tile([P, S], F32, name="first")
-        put_h1(0, first[:])
+        def deal(dst, src):
+            nc.vector.tensor_copy(
+                dst[:].rearrange("p a (b t q) -> p (a b) t q", b=2, t=PACK),
+                src[:].rearrange("p a (b q t) -> p (a b) t q", b=2, t=PACK),
+            )
+
+        v2_sc = held("v2_sc", [P, S], U8)
+        v2_w = held("v2_w", [P, S], U32)
+        nc.vector.tensor_copy(v2_w[:], tab2_w[:].indirect(idx2[:]))
+        nc.vector.tensor_copy(v2_sc[:], tab2_sc[:, 0, :].indirect(idx2[:]))
+        w1_w = held("w1_w", [P, 2, H], U16)
+        deal(w1_w, w1_raw)
         w2_q[0] = quantize_w2(0)
+        neg_rest = held("neg_rest", [P, 2, PACK], F32)
+        nc.vector.tensor_scalar(neg_rest[:], rest_t[:], -1.0, None, ALU.mult)
+        w1_sc = held("w2_grouped0", [P, 2, H], U8)
+        deal(w1_sc, w1_sc_raw)
+        first = keep.tile([P, S], F32, name="first")
+        put_h2(0, first[:])
+        v_w = [held("v_w%d" % a, [P, S], U32) for a in range(2)]
+        v_sc = [held("v_sc%d" % a, [P, S], U8) for a in range(2)]
+        nc.vector.tensor_copy(v_w[0][:], tab_w[0][:].indirect(idx[:]))
+        for a in range(2):
+            nc.vector.tensor_copy(v_sc[a][:], tab_sc[:, a, :].indirect(idx[:]))
+        nc.vector.tensor_copy(v_w[1][:], tab_w[1][:].indirect(idx[:]))
+        gi_bv = held("gi_bv", [P, 2, PACK], F32)
+        nc.vector.tensor_tensor(gi_bv[:], gi_t[:], bv_t[:], ALU.mult)
         picked = {}
 
         def put(s):
             h = area(s, 1)
-            if s == SLABS - 1:
-                put_h1(s, h[:, S:])
-            put_h2(s, h[:, :S])
-            if s + 1 < SLABS - 1:
-                put_h1(s + 1, h[:, S:])
+            own = s in (PACK, SLABS - 1)
+            if own:
+                put_h2(s, h[:, S:])
+            put_h1(s, h[:, :S])
+            if s + 1 not in (PACK, SLABS - 1, SLABS):
+                put_h2(s + 1, keep.tile([P, S], F32, name="first")[:] if own else h[:, S:])
 
         def fetch_slab(s):
             picked[s] = area(s, 0)
@@ -272,54 +277,66 @@ def tile_list_capsule_segment_reading_kernel(
 
         for s in range(2):
             put(s)
+            if s == 0:
+                w2_q[1] = quantize_w2(1)
             fetch_slab(s)
-        w2_q[1] = quantize_w2(1)
-        wa_q[0] = quantize_wa(0)
-        wa_q[1] = quantize_wa(1)
-        x_planes.append(held("x_planes1", [P, QUARTERS, PACK, QW], BF16))
-        bent_planes.append(held("bent_planes1", [P, QUARTERS, PACK, QW], BF16))
         for s in range(SLABS - 1):
             mag, bend = area(s, 1), fresh("bend")
             magnitude(picked[s], mag, 0, QUARTERS)
             if s + 2 < SLABS:
                 put(s + 2)
+            if s == 5:
+                weave_first_pass(3)
             features(s, mag, bend, 0, QUARTERS)
             if s + 2 < SLABS:
                 fetch_slab(s + 2)
-            for q in {3: [0, 1], 4: [2], 5: [3]}.get(s, []):
+            if s == 1:
+                wa_grouped = [round_wa(a) for a in range(2)]
+                x_planes.append(held("x_planes1", [P, QUARTERS, PACK, QW], BF16))
+                bent_planes.append(held("bent_planes1", [P, QUARTERS, PACK, QW], BF16))
+            for q in {3: [0, 1], 4: [2]}.get(s, []):
                 weave_first_pass(q)
 
+        wa_w = held("w1_w", [P, 2, N], U32)
+        wa_sc = held("wa_sc", [P, 2, N], U8)
+        for a in range(2):
+            nc.vector.quantize_mx(out=wa_w[:, a, :].bitcast(FP8X4), scales=wa_sc[:, a, :], in_=wa_grouped[a][:])
         out_v = out.rearrange("(n p) j -> p n j", p=P)
         last = SLABS - 1
         mag, bend = area(last, 1), fresh("bend")
 
-        def passes(acc, w_codes, w_scales, moving, pair, b):
+        def passes(acc, w_codes, w_scales, moving, pair, b, c0, width):
             for i in range(2):
                 cols = slice(P * (2 * pair + i), P * (2 * pair + i + 1))
                 nc.tensor.matmul_mx(
-                    out=acc[:, QW * i : QW * (i + 1)], lhsT=w_codes[:, cols].bitcast(FP8X4), lhsT_scale=w_scales[:, cols],
-                    rhs=moving[0][:].bitcast(FP8X4), rhs_scale=moving[1][:],
+                    out=acc[:, width * i : width * (i + 1)],
+                    lhsT=w_codes[:, cols].bitcast(FP8X4), lhsT_scale=w_scales[:, cols],
+                    rhs=moving[0][:, c0 : c0 + width].bitcast(FP8X4), rhs_scale=moving[1][:, c0 : c0 + width],
                     start=(b == 0 and i == 0), stop=(b == 1 and i == 1),
                 )
 
-        for q in range(QUARTERS):
-            ya = [bank(4 * (q % 2) + pair) for pair in range(2)]
-            yb = [bank(4 * (q % 2) + 2 + pair) for pair in range(2)]
+        res = [held("tab_w%d" % pair, [P, 2 * R], F32) for pair in range(2)]
+        pieces = [(q, 0, QW) for q in range(QUARTERS - 1)] + [(QUARTERS - 1, c0, QW // 2) for c0 in (0, QW // 2)]
+        for n, (q, c0, width) in enumerate(pieces):
+            ya = [bank(4 * (n % 2) + pair) for pair in range(2)]
+            yb = [bank(4 * (n % 2) + 2 + pair) for pair in range(2)]
             for pair in range(2):
-                passes(ya[pair], wa_q[0][0], wa_q[0][1], x_q[0, q], pair, 0)
-                passes(yb[pair], wb_w[0], wb_sc[:, 0, :], bent_q[0, q], pair, 0)
-            magnitude(picked[last], mag, q, q + 1)
-            features(last, mag, bend, q, q + 1)
-            x_q[1, q] = weave("x1_%d" % q, x_planes[1], q, nc.scalar.copy)
-            bent_q[1, q] = weave("b1_%d" % q, bent_planes[1], q, nc.vector.tensor_copy)
+                passes(ya[pair], wa_w[:, 0, :], wa_sc[:, 0, :], x_q[0, q], pair, 0, c0, width)
+                passes(yb[pair], wb_w[0], wb_sc[:, 0, :], bent_q[0, q], pair, 0, c0, width)
+            if c0 == 0:
+                magnitude(picked[last], mag, q, q + 1)
+                features(last, mag, bend, q, q + 1)
+            x_last = weave("x1_%d" % n, x_planes[1], q, nc.scalar.copy, c0, width)
+            bent_last = weave("b1_%d" % n, bent_planes[1], q, nc.vector.tensor_copy, c0, width)
             for pair in range(2):
-                passes(ya[pair], wa_q[1][0], wa_q[1][1], x_q[1, q], pair, 1)
-                passes(yb[pair], wb_w[1], wb_sc[:, 1, :], bent_q[1, q], pair, 1)
+                passes(ya[pair], wa_w[:, 1, :], wa_sc[:, 1, :], x_last, pair, 1, 0, width)
+                passes(yb[pair], wb_w[1], wb_sc[:, 1, :], bent_last, pair, 1, 0, width)
+            j0 = QW * q + c0
             for pair in range(2):
-                left = ring.tile([P, 2 * QW], F32, name="left")
-                nc.scalar.copy(left[:], ya[pair][:])
-                res = ring.tile([P, 2 * QW], F32, name="res", bufs=3)
-                nc.vector.tensor_tensor(res[:], yb[pair][:], left[:], ALU.max)
+                left = ring.tile([P, 2 * QW], F32, name="left", bufs=4)
+                nc.scalar.copy(left[:, : 2 * width], ya[pair][:, : 2 * width])
+                done = res[pair][:, 2 * j0 : 2 * (j0 + width)]
+                nc.vector.tensor_tensor(done, yb[pair][:, : 2 * width], left[:, : 2 * width], ALU.max)
                 nc.sync.dma_start(
-                    out_v[:, 2 * pair : 2 * pair + 2, QW * q : QW * (q + 1)], res[:].rearrange("p (n c) -> p n c", n=2)
+                    out_v[:, 2 * pair : 2 * pair + 2, j0 : j0 + width], done.rearrange("p (n c) -> p n c", n=2)
                 )

@@ -64,16 +64,16 @@ def tile_list_capsule_segment_reading_kernel(
             return t
 
         def load_rows(name, src):
-            t = held(name, [P, 2, PACK], F32)
-            nc.sync.dma_start(t[:], src.rearrange("(b p t) -> p b t", b=2, t=PACK))
+            t = held(name, [P, 2, 2 * PACK], F32)
+            nc.sync.dma_start(t[:, :, :PACK], src.rearrange("(b p t) -> p b t", b=2, t=PACK))
             return t
 
-        def load_wg(name, src, half):
-            t = held(name, [P, 2, S], F32)
-            rows = src.rearrange("(q t) j -> q t j", t=PACK)[:, 2 * half : 2 * half + 2, :]
+        def load_wg(name, src, t0, t1):
+            t = held(name, [P, t1 - t0, S], F32)
+            rows = src.rearrange("(q t) j -> q t j", t=PACK)[:, t0:t1, :]
             for quad in range(4):
                 nc.sync.dma_start(t[32 * quad : 32 * quad + 32, :, :], rows)
-            return t
+            return [t[:, i, :] for i in range(t1 - t0)]
 
         def load_page(s):
             t = pages.tile([P, T2], F32, name="page")
@@ -93,33 +93,33 @@ def tile_list_capsule_segment_reading_kernel(
         tab2_w = load_words("tab2_w", tab2_words[0])
         idx2 = load_list("idx2", offs2)
         load_scales(tab2_sc, tab2_scales)
-        w2_raw = [load_raw("w2_raw0", w2[:, :HALF])]
+        w2_raw = [load_raw("w2_raw%d" % i, w2[:, HALF * i : HALF * (i + 1)]) for i in range(2)]
         w1_raw = held("w1_raw", [P, 2, H], U16)
         nc.sync.dma_start(w1_raw[:].bitcast(I32), w1_words.rearrange("a p c -> p a c").bitcast(I32))
-        w2_raw.append(load_raw("w2_raw1", w2[:, HALF : 2 * HALF]))
         load_scales(w1_sc_raw, w1_scales)
         page = [load_page(0)]
         rest_t = load_rows("rest_t", rest)
         g2_t = load_rows("g2_t", g2)
         idx4 = load_list("idx4", offs4)
-        wg2_t = [load_wg("wg2_lo", wg2, 0)]
+        wg2_t = load_wg("wg2_0", wg2, 0, 1)
         tab_w = [load_words("tab_w0", tab_words[0])]
         idx = load_list("idx", offs)
-        load_scales(tab_sc, tab_scales)
         tab_w.append(load_words("tab_w1", tab_words[1]))
-        g1_t = load_rows("g1_t", g1)
+        load_scales(tab_sc, tab_scales)
+        wg2_t.extend(load_wg("wg2_1", wg2, 1, 2))
         page.append(load_page(1))
+        g1_t = load_rows("g1_t", g1)
         idx3 = load_list("idx3", offs3)
-        wg1_t = [load_wg("wg1_lo", wg1, 0)]
+        wg1_t = load_wg("wg1_lo", wg1, 0, 2)
         idx5 = load_list("idx5", offs5)
+        wg2_t.extend(load_wg("wg2_hi", wg2, 2, 4))
         w2_raw.append(load_raw("w2_raw2", w2[:, 2 * HALF : 3 * HALF]))
         w2_raw.append(load_raw("area0", w2[:, 3 * HALF :]))
         bv_t = load_rows("bv_t", bv)
         gi_t = load_rows("gi_t", gi)
         go_t = load_rows("go_t", go)
         page.append(load_page(2))
-        wg2_t.append(load_wg("wg2_hi", wg2, 1))
-        wg1_t.append(load_wg("wg1_hi", wg1, 1))
+        wg1_t.extend(load_wg("wg1_hi", wg1, 2, 4))
         page.append(load_page(3))
         wa_raw = [load_raw("x_planes1", wa[0:KP, :]), load_raw("bent_planes1", wa[KP : 2 * KP, :])]
         load_scales(wb_sc, wb_scales)
@@ -167,7 +167,7 @@ def tile_list_capsule_segment_reading_kernel(
                 )
             nc.scalar.activation(h1, acc[:], ACT.Copy, scale=col(g1_t, s))
             t = s % PACK
-            nc.vector.tensor_tensor(page[s][:].indirect(idx3[:]), h1, wg1_t[t // 2][:, t % 2, :], ALU.mult)
+            nc.vector.tensor_tensor(page[s][:].indirect(idx3[:]), h1, wg1_t[t], ALU.mult)
 
         def put_h2(s, h2):
             acc = next_bank()
@@ -178,10 +178,8 @@ def tile_list_capsule_segment_reading_kernel(
                 out=acc[:], lhsT=codes[:, cols].bitcast(FP8X4), lhsT_scale=scales[:, cols],
                 rhs=v2_w[:].bitcast(FP8X4), rhs_scale=v2_sc[:], start=True, stop=True,
             )
-            th = keep.tile([P, S], F32, name="th")
-            nc.scalar.activation(th[:], acc[:], ACT.Tanh, bias=col(neg_rest, s))
-            nc.scalar.activation(h2, th[:], ACT.Copy, scale=col(g2_t, s))
-            nc.vector.tensor_tensor(page[s][:].indirect(idx4[:]), h2, wg2_t[t // 2][:, t % 2, :], ALU.mult)
+            nc.scalar.activation(h2, acc[:], ACT.Tanh, bias=col(neg_rest, s))
+            nc.vector.tensor_tensor(page[s][:].indirect(idx4[:]), h2, gain2[s], ALU.mult)
 
         x_planes = [held("x_planes0", [P, QUARTERS, PACK, QW], BF16)]
         bent_planes = [held("bent_planes0", [P, QUARTERS, PACK, QW], BF16)]
@@ -244,11 +242,19 @@ def tile_list_capsule_segment_reading_kernel(
         deal(w1_w, w1_raw)
         w2_q[0] = quantize_w2(0)
         neg_rest = held("neg_rest", [P, 2, PACK], F32)
-        nc.vector.tensor_scalar(neg_rest[:], rest_t[:], -1.0, None, ALU.mult)
+        nc.vector.tensor_scalar(neg_rest[:], rest_t[:, :, :PACK], -1.0, None, ALU.mult)
         w1_sc = held("w2_grouped0", [P, 2, H], U8)
         deal(w1_sc, w1_sc_raw)
+        gain2 = {}
+
+        def fold_g2(s):
+            gain2[s] = held("gain2_%d" % s, [P, S], F32)[:] if s < PACK else wg2_t[s - PACK]
+            nc.scalar.activation(gain2[s], wg2_t[s % PACK], ACT.Copy, scale=col(g2_t, s))
+
+        fold_g2(0)
         first = keep.tile([P, S], F32, name="first")
         put_h2(0, first[:])
+        fold_g2(1)
         v_w = [held("v_w%d" % a, [P, S], U32) for a in range(2)]
         v_sc = [held("v_sc%d" % a, [P, S], U8) for a in range(2)]
         nc.vector.tensor_copy(v_w[0][:], tab_w[0][:].indirect(idx[:]))
@@ -256,8 +262,8 @@ def tile_list_capsule_segment_reading_kernel(
             nc.vector.tensor_copy(v_sc[a][:], tab_sc[:, a, :].indirect(idx[:]))
         nc.vector.tensor_copy(v_w[1][:], tab_w[1][:].indirect(idx[:]))
         gi_bv = held("gi_bv", [P, 2, PACK], F32)
-        nc.vector.tensor_tensor(gi_bv[:], gi_t[:], bv_t[:], ALU.mult)
-        picked = {}
+        nc.vector.tensor_tensor(gi_bv[:], gi_t[:, :, :PACK], bv_t[:, :, :PACK], ALU.mult)
+        picked, wa_grouped = {}, []
 
         def put(s):
             h = area(s, 1)
@@ -278,6 +284,8 @@ def tile_list_capsule_segment_reading_kernel(
         for s in range(2):
             put(s)
             if s == 0:
+                for later in range(2, SLABS):
+                    fold_g2(later)
                 w2_q[1] = quantize_w2(1)
             fetch_slab(s)
         for s in range(SLABS - 1):
@@ -290,8 +298,9 @@ def tile_list_capsule_segment_reading_kernel(
             features(s, mag, bend, 0, QUARTERS)
             if s + 2 < SLABS:
                 fetch_slab(s + 2)
-            if s == 1:
-                wa_grouped = [round_wa(a) for a in range(2)]
+            if s in (1, 2):
+                wa_grouped.append(round_wa(s - 1))
+            if s == 2:
                 x_planes.append(held("x_planes1", [P, QUARTERS, PACK, QW], BF16))
                 bent_planes.append(held("bent_planes1", [P, QUARTERS, PACK, QW], BF16))
             for q in {3: [0, 1], 4: [2]}.get(s, []):

from contextlib import ExitStack

import concourse.mybir as mybir

K, K2, H, N, T, T3, S, T2, R = 1024, 512, 1024, 512, 2048, 1024, 512, 2048, 1024
FLOPS = 2 * S * H * (K + K2) + 2 * 2 * H * N * R

F32 = mybir.dt.float32
BF16 = mybir.dt.bfloat16
I32 = mybir.dt.int32
U32 = mybir.dt.uint32
U16 = mybir.dt.uint16
U8 = mybir.dt.uint8
FP8X4 = mybir.dt.float8_e4m3fn_x4
FP4X4 = mybir.dt.float4_e2m1fn_x4
ACT = mybir.ActivationFunctionType
ALU = mybir.AluOpType

P = 128
PACK = 4
KP = P * PACK
SLABS = H // P
QW = 256
QUARTERS = R // QW
RUN = 4
HALF = KP // 2


def tile_list_capsule_segment_reading_kernel(
    tc, tab_words, tab_scales, offs, tab2_words, tab2_scales, offs2, w1_words, w1_scales, g1, w2, rest, g2,
    page0, offs3, offs4, wg1, wg2, offs5, bv, gi, go, wa, wb_words, wb_scales, out,
):
    nc = tc.nc
    with ExitStack() as ctx:
        keep = ctx.enter_context(tc.tile_pool(name="keep", bufs=1))
        ring = ctx.enter_context(tc.tile_pool(name="ring", bufs=2))
        pages = ctx.enter_context(tc.tile_pool(name="pages", bufs=4))
        psum = ctx.enter_context(tc.psum_pool(name="psum", bufs=1))

        def held(name, shape, dtype):
            return keep.tile(shape, dtype, name=name, align_bytes=64)

        def bank(i):
            return psum.tile([P, 512], F32, name="bank%d" % i)

        def load_list(name, src):
            t = keep.tile(list(src.shape), U16, name=name)
            nc.sync.dma_start(t[:], src)
            return t

        def scale_tile(name, src, engine):
            t = held(name, [P, src.shape[0], src.shape[2]], U8)
            engine.memset(t[:].bitcast(I32), 0)
            return t

        def load_scales(t, src):
            rows = src.bitcast(I32).rearrange("a (q r) c -> r q a c", r=4)
            for r in range(4):
                nc.sync.dma_start(t[r:P:32, :, :].bitcast(I32), rows[r])

        def load_words(name, src):
            t = held(name, [P, src.shape[1]], U32)
            nc.sync.dma_start(t[:].bitcast(I32), src.rearrange("p n i -> p (n i)").bitcast(I32))
            return t

        def load_rows(name, src):
            t = held(name, [P, 2, 2 * PACK], F32)
            nc.sync.dma_start(t[:, :, :PACK], src.rearrange("(b p t) -> p b t", b=2, t=PACK))
            return t

        def load_wg(name, src, t0, t1):
            t = held(name, [P, t1 - t0, S], F32)
            rows = src.rearrange("(q t) j -> q t j", t=PACK)[:, t0:t1, :]
            for quad in range(4):
                nc.sync.dma_start(t[32 * quad : 32 * quad + 32, :, :], rows)
            return [t[:, i, :] for i in range(t1 - t0)]

        def load_page(s):
            t = pages.tile([P, T2], F32, name="page")
            nc.sync.dma_start(t[:], page0.rearrange("(b p t) c -> b t p c", b=2, t=PACK)[s // PACK, s % PACK])
            return t

        def load_raw(name, src):
            t = held(name, [P, PACK, src.shape[1]], F32)
            nc.sync.dma_start(t[:], src.rearrange("(p j) c -> p j c", j=PACK))
            return t

        tab2_sc = scale_tile("tab2_sc", tab2_scales, nc.vector)
        w1_sc_raw = scale_tile("w1_sc_raw", w1_scales, nc.vector)
        tab_sc = scale_tile("tab_sc", tab_scales, nc.gpsimd)
        wb_sc = scale_tile("wb_sc", wb_scales, nc.gpsimd)

        tab2_w = load_words("tab2_w", tab2_words[0])
        idx2 = load_list("idx2", offs2)
        load_scales(tab2_sc, tab2_scales)
        w2_raw = [load_raw("w2_raw%d" % i, w2[:, HALF * i : HALF * (i + 1)]) for i in range(2)]
        w1_raw = held("w1_raw", [P, 2, H], U16)
        nc.sync.dma_start(w1_raw[:].bitcast(I32), w1_words.rearrange("a p c -> p a c").bitcast(I32))
        load_scales(w1_sc_raw, w1_scales)
        page = [load_page(0)]
        rest_t = load_rows("rest_t", rest)
        g2_t = load_rows("g2_t", g2)
        idx4 = load_list("idx4", offs4)
        wg2_t = load_wg("wg2_0", wg2, 0, 1)
        tab_w = [load_words("tab_w0", tab_words[0])]
        idx = load_list("idx", offs)
        tab_w.append(load_words("tab_w1", tab_words[1]))
        load_scales(tab_sc, tab_scales)
        wg2_t.extend(load_wg("wg2_1", wg2, 1, 2))
        page.append(load_page(1))
        g1_t = load_rows("g1_t", g1)
        idx3 = load_list("idx3", offs3)
        wg1_t = load_wg("wg1_lo", wg1, 0, 2)
        idx5 = load_list("idx5", offs5)
        wg2_t.extend(load_wg("wg2_hi", wg2, 2, 4))
        w2_raw.append(load_raw("w2_raw2", w2[:, 2 * HALF : 3 * HALF]))
        w2_raw.append(load_raw("area0", w2[:, 3 * HALF :]))
        bv_t = load_rows("bv_t", bv)
        gi_t = load_rows("gi_t", gi)
        go_t = load_rows("go_t", go)
        page.append(load_page(2))
        wg1_t.extend(load_wg("wg1_hi", wg1, 2, 4))
        page.append(load_page(3))
        wa_raw = [load_raw("x_planes1", wa[0:KP, :]), load_raw("bent_planes1", wa[KP : 2 * KP, :])]
        load_scales(wb_sc, wb_scales)
        wb_w = [load_words("wb_w%d" % a, wb_words[a]) for a in range(2)]

        def col(t, s):
            return t[:, s // PACK, s % PACK : s % PACK + 1]

        def quantize(name, grouped, width):
            codes = held(name + "_w", [P, width], U32)
            scales = held(name + "_sc", [P, width], U8)
            nc.vector.quantize_mx(out=codes[:].bitcast(FP8X4), scales=scales[:], in_=grouped)
            return codes, scales

        def quantize_w2(b):
            grouped = held("w2_grouped%d" % b, [P, PACK * KP], BF16)
            for i in range(2):
                nc.scalar.copy(
                    grouped[:].rearrange("p (t i m j) -> p i m j t", t=PACK, i=2, j=PACK)[:, i],
                    w2_raw[2 * b + i][:].rearrange("p j (m t) -> p m j t", t=PACK),
                )
            return quantize("w2_%d" % b, grouped[:], KP)

        def round_wa(a):
            grouped = held("wa_grouped%d" % a, [P, PACK * KP], BF16)
            nc.scalar.copy(
                grouped[:].rearrange("p (c i j) -> p c j i", i=RUN, j=PACK),
                wa_raw[a][:].rearrange("p j (c i) -> p c j i", i=RUN),
            )
            return grouped

        turn = [0]

        def next_bank():
            turn.append(turn[-1] + 1)
            return bank(turn[-1] % 4)

        def put_h1(s, h1):
            acc = next_bank()
            cols = slice(P * s, P * s + P)
            for a in range(2):
                nc.tensor.matmul_mx(
                    out=acc[:], lhsT=w1_w[:, a, cols].bitcast(FP4X4), lhsT_scale=w1_sc[:, a, cols],
                    rhs=v_w[a][:].bitcast(FP8X4), rhs_scale=v_sc[a][:], start=(a == 0), stop=(a == 1),
                )
            nc.scalar.activation(h1, acc[:], ACT.Copy, scale=col(g1_t, s))
            t = s % PACK
            nc.vector.tensor_tensor(page[s][:].indirect(idx3[:]), h1, wg1_t[t], ALU.mult)

        def put_h2(s, h2):
            acc = next_bank()
            t = s % PACK
            codes, scales = w2_q[s // PACK]
            cols = slice(P * t, P * t + P)
            nc.tensor.matmul_mx(
                out=acc[:], lhsT=codes[:, cols].bitcast(FP8X4), lhsT_scale=scales[:, cols],
                rhs=v2_w[:].bitcast(FP8X4), rhs_scale=v2_sc[:], start=True, stop=True,
            )
            nc.scalar.activation(h2, acc[:], ACT.Tanh, bias=col(neg_rest, s))
            nc.vector.tensor_tensor(page[s][:].indirect(idx4[:]), h2, gain2[s], ALU.mult)

        x_planes = [held("x_planes0", [P, QUARTERS, PACK, QW], BF16)]
        bent_planes = [held("bent_planes0", [P, QUARTERS, PACK, QW], BF16)]

        def fetch(s, picked, q0, q1):
            nc.vector.tensor_copy(
                picked[:, QW * q0 : QW * q1], page[s][:].indirect(idx5[:, QW // 16 * q0 : QW // 16 * q1])
            )

        def magnitude(picked, mag, q0, q1):
            nc.scalar.activation(mag[:, QW * q0 : QW * q1], picked[:, QW * q0 : QW * q1], ACT.Abs)

        def features(s, mag, bend, q0, q1):
            b, t = divmod(s, PACK)
            cols = slice(QW * q0, QW * q1)
            if s == SLABS - 1 and q0 > 0:
                nc.vector.tensor_scalar(x_planes[b][:, q0, t, :], mag[:, cols], col(bv_t, s), None, ALU.add)
            else:
                nc.scalar.activation(
                    x_planes[b][:, q0:q1, t, :], mag[:, cols].rearrange("p (q c) -> p q c", c=QW), ACT.Identity,
                    bias=col(bv_t, s),
                )
            nc.scalar.activation(bend[:, cols], mag[:, cols], ACT.Tanh, bias=col(gi_bv, s), scale=col(gi_t, s))
            nc.scalar.activation(
                bent_planes[b][:, q0:q1, t, :], bend[:, cols].rearrange("p (q c) -> p q c", c=QW), ACT.Copy,
                scale=col(go_t, s),
            )

        def weave(name, planes, q, copy, c0=0, width=QW):
            grouped = ring.tile([P, PACK * QW], BF16, name="grouped_" + name[0], align_bytes=64, bufs=4)
            copy(
                grouped[:, : PACK * width].rearrange("p (c i t) -> p c t i", i=RUN, t=PACK),
                planes[:, q, :, c0 : c0 + width].rearrange("p t (c i) -> p c t i", i=RUN),
            )
            return quantize(name, grouped[:, : PACK * width], width)

        x_q, bent_q, w2_q = {}, {}, {}

        def weave_first_pass(q):
            x_q[0, q] = weave("x0_%d" % q, x_planes[0], q, nc.scalar.copy)
            bent_q[0, q] = weave("b0_%d" % q, bent_planes[0], q, nc.scalar.copy)

        def fresh(name):
            return held(name, [P, R], F32)

        def area(s, role):
            return fresh("area%d" % (2 * (s % 2) + (s // 2 + role) % 2))

        def deal(dst, src):
            nc.vector.tensor_copy(
                dst[:].rearrange("p a (b t q) -> p (a b) t q", b=2, t=PACK),
                src[:].rearrange("p a (b q t) -> p (a b) t q", b=2, t=PACK),
            )

        v2_sc = held("v2_sc", [P, S], U8)
        v2_w = held("v2_w", [P, S], U32)
        nc.vector.tensor_copy(v2_w[:], tab2_w[:].indirect(idx2[:]))
        nc.vector.tensor_copy(v2_sc[:], tab2_sc[:, 0, :].indirect(idx2[:]))
        w1_w = held("w1_w", [P, 2, H], U16)
        deal(w1_w, w1_raw)
        w2_q[0] = quantize_w2(0)
        neg_rest = held("neg_rest", [P, 2, PACK], F32)
        nc.vector.tensor_scalar(neg_rest[:], rest_t[:, :, :PACK], -1.0, None, ALU.mult)
        w1_sc = held("w2_grouped0", [P, 2, H], U8)
        deal(w1_sc, w1_sc_raw)
        gain2 = {}

        def fold_g2(s):
            gain2[s] = held("gain2_%d" % s, [P, S], F32)[:] if s < PACK else wg2_t[s - PACK]
            nc.scalar.activation(gain2[s], wg2_t[s % PACK], ACT.Copy, scale=col(g2_t, s))

        fold_g2(0)
        first = keep.tile([P, S], F32, name="first")
        put_h2(0, first[:])
        fold_g2(1)
        v_w = [held("v_w%d" % a, [P, S], U32) for a in range(2)]
        v_sc = [held("v_sc%d" % a, [P, S], U8) for a in range(2)]
        nc.vector.tensor_copy(v_w[0][:], tab_w[0][:].indirect(idx[:]))
        for a in range(2):
            nc.vector.tensor_copy(v_sc[a][:], tab_sc[:, a, :].indirect(idx[:]))
        nc.vector.tensor_copy(v_w[1][:], tab_w[1][:].indirect(idx[:]))
        gi_bv = held("gi_bv", [P, 2, PACK], F32)
        nc.vector.tensor_tensor(gi_bv[:], gi_t[:, :, :PACK], bv_t[:, :, :PACK], ALU.mult)
        picked, wa_grouped = {}, []

        def put(s):
            h = area(s, 1)
            own = s in (PACK, SLABS - 1)
            if own:
                put_h2(s, h[:, S:])
            put_h1(s, h[:, :S])
            if s + 1 not in (PACK, SLABS - 1, SLABS):
                put_h2(s + 1, keep.tile([P, S], F32, name="first")[:] if own else h[:, S:])

        def fetch_slab(s):
            picked[s] = area(s, 0)
            for q0, q1 in [(0, QUARTERS)] if s < SLABS - 1 else [(q, q + 1) for q in range(QUARTERS)]:
                fetch(s, picked[s], q0, q1)
            if s + 4 < SLABS:
                page.append(load_page(s + 4))

        for s in range(2):
            put(s)
            if s == 0:
                for later in range(2, SLABS):
                    fold_g2(later)
                w2_q[1] = quantize_w2(1)
            fetch_slab(s)
        for s in range(SLABS - 1):
            mag, bend = area(s, 1), fresh("bend")
            magnitude(picked[s], mag, 0, QUARTERS)
            if s + 2 < SLABS:
                put(s + 2)
            if s == 5:
                weave_first_pass(3)
            features(s, mag, bend, 0, QUARTERS)
            if s + 2 < SLABS:
                fetch_slab(s + 2)
            if s in (1, 2):
                wa_grouped.append(round_wa(s - 1))
            if s == 2:
                x_planes.append(held("x_planes1", [P, QUARTERS, PACK, QW], BF16))
                bent_planes.append(held("bent_planes1", [P, QUARTERS, PACK, QW], BF16))
            for q in {3: [0, 1], 4: [2]}.get(s, []):
                weave_first_pass(q)

        wa_w = held("w1_w", [P, 2, N], U32)
        wa_sc = held("wa_sc", [P, 2, N], U8)
        for a in range(2):
            nc.vector.quantize_mx(out=wa_w[:, a, :].bitcast(FP8X4), scales=wa_sc[:, a, :], in_=wa_grouped[a][:])
        out_v = out.rearrange("(n p) j -> p n j", p=P)
        last = SLABS - 1
        mag, bend = area(last, 1), fresh("bend")

        def passes(acc, w_codes, w_scales, moving, pair, b, c0, width):
            for i in range(2):
                cols = slice(P * (2 * pair + i), P * (2 * pair + i + 1))
                nc.tensor.matmul_mx(
                    out=acc[:, width * i : width * (i + 1)],
                    lhsT=w_codes[:, cols].bitcast(FP8X4), lhsT_scale=w_scales[:, cols],
                    rhs=moving[0][:, c0 : c0 + width].bitcast(FP8X4), rhs_scale=moving[1][:, c0 : c0 + width],
                    start=(b == 0 and i == 0), stop=(b == 1 and i == 1),
                )

        res = [held("tab_w%d" % pair, [P, 2 * R], F32) for pair in range(2)]
        pieces = [(q, 0, QW) for q in range(QUARTERS - 1)] + [(QUARTERS - 1, c0, QW // 2) for c0 in (0, QW // 2)]
        for n, (q, c0, width) in enumerate(pieces):
            ya = [bank(4 * (n % 2) + pair) for pair in range(2)]
            yb = [bank(4 * (n % 2) + 2 + pair) for pair in range(2)]
            for pair in range(2):
                passes(ya[pair], wa_w[:, 0, :], wa_sc[:, 0, :], x_q[0, q], pair, 0, c0, width)
                passes(yb[pair], wb_w[0], wb_sc[:, 0, :], bent_q[0, q], pair, 0, c0, width)
            if c0 == 0:
                magnitude(picked[last], mag, q, q + 1)
                features(last, mag, bend, q, q + 1)
            x_last = weave("x1_%d" % n, x_planes[1], q, nc.scalar.copy, c0, width)
            bent_last = weave("b1_%d" % n, bent_planes[1], q, nc.vector.tensor_copy, c0, width)
            for pair in range(2):
                passes(ya[pair], wa_w[:, 1, :], wa_sc[:, 1, :], x_last, pair, 1, 0, width)
                passes(yb[pair], wb_w[1], wb_sc[:, 1, :], bent_last, pair, 1, 0, width)
            j0 = QW * q + c0
            for pair in range(2):
                left = ring.tile([P, 2 * QW], F32, name="left", bufs=4)
                nc.scalar.copy(left[:, : 2 * width], ya[pair][:, : 2 * width])
                done = res[pair][:, 2 * j0 : 2 * (j0 + width)]
                nc.vector.tensor_tensor(done, yb[pair][:, : 2 * width], left[:, : 2 * width], ALU.max)
                nc.sync.dma_start(
                    out_v[:, 2 * pair : 2 * pair + 2, j0 : j0 + width], done.rearrange("p (n c) -> p n c", n=2)
                )
